import numpy as np
CORES = [0,1,2,3,4,5,6,7,8,9,10,11,12,13,14,15,16,17,18,19,20,21,22,23,24,25,26,27,28,29,30,31,32,33,34,35,36,37,38,39,40,41,42,43,44,45,46,47,48,49,50,51,52,53,54,55,56,57,58,59,60,61,62,63,64,65,66,67,68,69,70,71,72,73,74,75,76,77,78,79,80,81,82,83,84,85,86,87,88,89,90,91,92,93,94,95,96,97,98,99,100,101,102,103,104,105,106,107,108,109,110,111,112,113,114,115,116,117,118,119,120,121,122,123,124,125,126,127,168,169,170,171,172,173,174,175]
N = 136
def setup_inputs(rng):
    return {"x": rng.standard_normal((N, 128, 1024), dtype=np.float32)}
def reference(x):
    s = x.sum(axis=0, dtype=np.float64).astype(x.dtype)
    return {"y": np.broadcast_to(s, (N,) + s.shape)}

from concourse.bass import DstId, RemoteDMATransfer

BLOCK, PIECE = 128, 16
A = (2, 3, 6, 7)
B = (0, 1, 4, 5)
X_HOST, X_CHIP, RELAY_CHIP = 1, 5, 4

SCRATCH = {
    "xs": ("sbuf", [128, 8 * BLOCK], "float32"),
    "chipl": ("sbuf", [128, 7 * BLOCK], "float32"),
    "matel": ("sbuf", [128, BLOCK], "float32"),
    "planel": ("sbuf", [128, 8 * PIECE], "float32"),
    "res": ("sbuf", [128, 8 * BLOCK], "float32"),
}
SEMAPHORES = ["loaded", "chip", "mate", "plane", "piece", "block", "final", "sent", "stored"]

OFF_CHIP = 0x00FF
UPPER = 0xFF00
ALL = 0xFFFF


def world(host, chip, k):
    return host * 128 + chip * 8 + k


def engines(mask):
    return bin(mask).count("1")


def rank_program(g, core, T, topo):
    host, chip, k = topo.host(core), topo.chip(core), core % 8
    on_x = host == X_HOST and chip == X_CHIP
    relay = host == X_HOST and chip == RELAY_CHIP and k in A
    if not (host == 0 or on_x or relay):
        return
    sem = T.sem
    sent = [0]

    def transfer(mask, remote_sem, srcs, dsts):
        ids = []
        for d, ap in dsts:
            rid, pid = topo.addr(d, core)
            ids.append(DstId(rid=rid, pnc=pid))
        sent[0] += engines(mask)
        return RemoteDMATransfer(dst_ids=ids, dma_engine_mask=mask, remote_sem=remote_sem, srcs=list(srcs),
                                 dsts=[ap for d, ap in dsts], alu_op=1 if len(srcs) > 1 else 0)

    def issue(transfers):
        g.remote_dma_fused(transfers, local_sem=sem.sent)

    def cols(h, t, q=None):
        lo = (4 * h + t) * BLOCK
        return slice(lo, lo + BLOCK) if q is None else slice(lo + q * PIECE, lo + (q + 1) * PIECE)

    if relay:
        t = A.index(k)
        g.wait_ge(sem.piece, 8 * engines(OFF_CHIP))
        issue([transfer(OFF_CHIP, sem.block, [T.matel[:, :]], [(world(X_HOST, X_CHIP, A[t]), T.res[:, cols(0, t)])])])
        g.wait_ge(sem.sent, sent[0])
        return

    p, q = chip % 2, chip // 2
    is_a = k in A
    t = A.index(k) if is_a else B.index(k)
    others = [j for j in range(8) if j != k]

    def half_of(j):
        return 1 - p if j in A else p

    def index_of(j):
        return A.index(j) if j in A else B.index(j)

    mine = half_of(k)

    def copies(part):
        lo = (4 * mine + t) * BLOCK
        own = T.xs[:, lo + part.start:lo + part.stop]
        return [own] + [T.chipl[:, s * BLOCK + part.start:s * BLOCK + part.stop] for s in range(7)]

    def piece(i):
        return slice(i * PIECE, (i + 1) * PIECE)

    def broadcast(h, mask):
        return transfer(mask, sem.final, [T.res[:, cols(h, t)]],
                        [(world(host, chip, j), T.res[:, cols(h, t)]) for j in others])

    g.dma_start(T.xs[:, :], T.x[:, :]).then_inc(sem.loaded, 16)
    g.wait_ge(sem.loaded, 16)

    issue([transfer(3 << (2 * n), sem.chip, [T.xs[:, cols(half_of(j), index_of(j))]],
                    [(world(host, chip, j), T.chipl[:, (k - (k > j)) * BLOCK:(k - (k > j) + 1) * BLOCK])])
           for n, j in enumerate(others)])
    g.wait_ge(sem.chip, 7 * 2)

    if on_x:
        issue([transfer(1 << i, sem.plane, copies(piece(i)),
                        [(world(0, 2 * i + mine, B[t]), T.planel[:, 7 * PIECE:8 * PIECE])]) for i in range(8)])
        if is_a:
            g.wait_ge(sem.block, engines(OFF_CHIP))
        else:
            g.wait_ge(sem.piece, 8 * engines(OFF_CHIP))
        issue([broadcast(mine, ALL)])
        g.wait_ge(sem.final, 7 * engines(ALL))
    elif is_a:
        mate_b = world(0, chip ^ 1, B[t])
        issue([transfer(OFF_CHIP, sem.mate, copies(slice(0, BLOCK)), [(mate_b, T.matel[:, :])])])
        g.wait_ge(sem.piece, 8 * engines(OFF_CHIP))
        issue([transfer(OFF_CHIP, sem.block, [T.res[:, cols(p, t)]], [(mate_b, T.res[:, cols(p, t)])]),
               broadcast(p, UPPER)])
        g.wait_ge(sem.final, 3 * engines(UPPER) + 4 * engines(ALL))
    else:
        g.wait_ge(sem.mate, engines(OFF_CHIP))
        peers = [i for i in range(8) if i != q]
        issue([transfer(1 << n, sem.plane, copies(piece(i)) + [T.matel[:, piece(i)]],
                        [(world(0, 2 * i + p, k), T.planel[:, piece(q - (q > i))])]) for n, i in enumerate(peers)])
        g.wait_ge(sem.plane, 8)
        place = T.res[:, cols(p, t, q)]
        dsts = [(world(0, 2 * i + p, A[t]), place) for i in range(8)]
        if p == X_CHIP % 2:
            dsts.append((world(X_HOST, X_CHIP, B[t]), place))
        else:
            dsts.append((world(X_HOST, RELAY_CHIP, A[t]), T.matel[:, piece(q)]))
        issue([transfer(OFF_CHIP, sem.piece,
                        copies(piece(q)) + [T.matel[:, piece(q)]] + [T.planel[:, piece(s)] for s in range(8)], dsts)])
        g.wait_ge(sem.block, engines(OFF_CHIP))
        issue([broadcast(1 - p, ALL)])
        g.wait_ge(sem.final, 4 * engines(UPPER) + 3 * engines(ALL))

    g.dma_start(T.y[:, :], T.res[:, :]).then_inc(sem.stored, 16)
    g.wait_ge(sem.stored, 16)
    g.wait_ge(sem.sent, sent[0])
